import numpy as np
import ml_dtypes


def mxq(x, axis, fmt="e4m3"):
    dtype, down = {"e4m3": (ml_dtypes.float8_e4m3fn, 7), "e5m2": (ml_dtypes.float8_e5m2, 14)}[fmt]
    v = np.moveaxis(np.asarray(x, np.float32).astype(ml_dtypes.bfloat16).astype(np.float64), axis, -1)
    blocks = v.reshape(v.shape[:-1] + (-1, 32))
    amax = np.abs(blocks).max(-1, keepdims=True)
    byte = np.maximum(np.where(amax > 0, np.frexp(amax)[1] - 1 + 127, 0) - down, 1)
    scale = np.exp2(byte - 127.0)
    codes = (blocks / scale).astype(np.float32).astype(dtype).astype(np.float64)
    return np.moveaxis((codes * scale).reshape(v.shape), -1, axis)


WIDE = False


def mx_kscale(k):
    if not WIDE:
        return np.ones(k)
    levels = np.array([30, -30])
    if k % 512:
        return np.exp2(np.random.permutation(np.resize(levels, k // 32))).repeat(32)
    a = np.empty((k // 512, 16))
    for p in range(k // 512):
        a[p, :8] = np.random.permutation(np.resize(levels, 8))
        for g in range(8):
            far = levels[np.abs(levels - a[p, g]) >= 10]
            a[p, g + 8] = far[np.random.randint(len(far))]
    return np.exp2(a.ravel()).repeat(32)


def f64(x):
    return np.asarray(x).astype(np.float64)


def striped(idx):
    return np.tile(np.asarray(idx).reshape(-1, 16).T, (8, 1)).astype(np.uint16)


def unstriped(offs):
    return offs[:16].T.reshape(-1).astype(np.int64)


E2M1 = np.array([0.0, 0.5, 1.0, 1.5, 2.0, 3.0, 4.0, 6.0, -0.0, -0.5, -1.0, -1.5, -2.0, -3.0, -4.0, -6.0])


def pack_weight(w, fmt):
    k, n = w.shape
    w = f64(np.asarray(w, np.float32).astype(ml_dtypes.bfloat16)).reshape(k // 32, 32, n)
    amax = np.abs(w).max(1)
    if fmt in ("e4m3", "e5m2"):
        byte = np.frexp(amax)[1] - 1 + 127 - (7 if fmt == "e4m3" else 14)
    else:
        mant, ex = np.frexp(amax / 6.0)
        byte = np.where(mant > 0.5, ex, ex - 1) + 127
    byte = np.clip(np.where(amax > 0, byte, 1), 1, 254)
    scaled = (w * np.exp2(127.0 - byte)[:, None, :]).reshape(k, n).astype(np.float32)
    by_word = np.ascontiguousarray(scaled.reshape(k // 512, 128, 4, n).transpose(0, 1, 3, 2))
    if fmt in ("e4m3", "e5m2"):
        words = by_word.astype(ml_dtypes.float8_e4m3fn if fmt == "e4m3" else ml_dtypes.float8_e5m2).view(np.uint8)
    else:
        c = by_word.astype(ml_dtypes.float4_e2m1fn).view(np.uint8) & 0xF
        words = (c[..., 0::2] | (c[..., 1::2] << 4)).reshape(k // 512, 128, 2 * n)
    return np.ascontiguousarray(words), np.ascontiguousarray(byte.astype(np.uint8).reshape(k // 512, 16, n))


def unpack_weight(words, scales, fmt):
    g, _, n = scales.shape
    words = np.ascontiguousarray(words).reshape(g, 128, n, -1)
    if fmt in ("e4m3", "e5m2"):
        vals = words.view(ml_dtypes.float8_e4m3fn if fmt == "e4m3" else ml_dtypes.float8_e5m2).astype(np.float64)
    else:
        nib = np.empty((g, 128, n, 4), np.uint8)
        nib[..., 0::2] = words & 0xF
        nib[..., 1::2] = words >> 4
        vals = E2M1[nib]
    vals = vals * np.repeat(np.exp2(scales.astype(np.float64) - 127.0), 8, axis=1)[..., None]
    return vals.transpose(0, 1, 3, 2).reshape(g * 512, n)


def sigmoid(v):
    return 1.0 / (1.0 + np.exp(-v))


K, F, T, Z, J, R, O, N, E = 512, 512, 1024, 1024, 256, 512, 128, 256, 1024


def setup_inputs():
    n = np.random.standard_normal
    idx = np.random.permutation(T)[:J]
    idx2 = np.random.permutation(Z)[:J]
    idx3 = np.random.permutation(J)[:J]
    idx4 = np.random.permutation(J)[:O]
    idx5 = np.random.permutation(J)[:O]
    idx6 = np.random.permutation(E)[:O]
    fk = mx_kscale(K)
    ff = mx_kscale(F)
    fr = mx_kscale(R)
    xtp = pack_weight(n((K, T)) / fk[:, None], "e2m1")
    wp = pack_weight(n((K, R)) * 1 / np.sqrt(K) * fk[:, None], "e5m2")
    xop = pack_weight(n((F, Z)) / ff[:, None], "e5m2")
    w2p = pack_weight(n((F, R)) * 1 / np.sqrt(F) * ff[:, None] * fr, "e4m3")
    wbp = pack_weight(n((R, N)) * 1 / np.sqrt(R) / fr[:, None], "e4m3")
    return {
        "xt_words": xtp[0],
        "xt_scales": xtp[1],
        "w_words": wp[0],
        "w_scales": wp[1],
        "xo_words": xop[0],
        "xo_scales": xop[1],
        "w2_words": w2p[0],
        "w2_scales": w2p[1],
        "sg": (np.random.uniform(0.6, 1.6, (R, 1))).astype(np.float32),
        "bg": (np.random.uniform(-1.0, 1.0, (R, 1))).astype(np.float32),
        "wb_words": wbp[0],
        "wb_scales": wbp[1],
        "tz": (n((N, E))).astype(np.float32),
        "offs": striped(idx),
        "offs2": striped(idx2),
        "offs3": striped(idx3),
        "offs4": striped(idx4),
        "offs5": striped(idx5),
        "offs6": striped(idx6),
    }


def reference(xt_words, xt_scales, w_words, w_scales, xo_words, xo_scales, w2_words, w2_scales, sg, bg, wb_words, wb_scales, tz, offs, offs2, offs3, offs4, offs5, offs6):
    idx = unstriped(offs)
    idx2 = unstriped(offs2)
    idx3 = unstriped(offs3)
    idx4 = unstriped(offs4)
    idx5 = unstriped(offs5)
    idx6 = unstriped(offs6)
    xtu = unpack_weight(xt_words, xt_scales, "e2m1")
    wu = unpack_weight(w_words, w_scales, "e5m2")
    xou = unpack_weight(xo_words, xo_scales, "e5m2")
    w2u = unpack_weight(w2_words, w2_scales, "e4m3")
    wbu = unpack_weight(wb_words, wb_scales, "e4m3")
    xtidxg = xtu[:, idx]
    a = wu.T @ xtidxg
    xoidx2g = xou[:, idx2]
    b = w2u.T @ xoidx2g
    hg = b * sigmoid(a[:, idx3] * f64(sg) + f64(bg))
    hid = np.maximum(hg[:, idx4], hg[:, idx5])
    hidq = mxq(hid, 0, "e5m2")
    p = wbu.T @ hidq
    y = p + f64(tz)[:, idx6]
    return y

@@ -1,0 +1,190 @@
+from contextlib import ExitStack
+
+import concourse.mybir as mybir
+
+K, F, T, Z, J, R, O, N, E = 512, 512, 1024, 1024, 256, 512, 128, 256, 1024
+FLOPS = 2 * K * R * J + 2 * F * R * J + 2 * R * N * O
+
+F32 = mybir.dt.float32
+BF16 = mybir.dt.bfloat16
+I32 = mybir.dt.int32
+U32 = mybir.dt.uint32
+U16 = mybir.dt.uint16
+U8 = mybir.dt.uint8
+E4M3 = mybir.dt.float8_e4m3fn_x4
+E5M2 = mybir.dt.float8_e5m2_x4
+E2M1 = mybir.dt.float4_e2m1fn_x4
+ACT = mybir.ActivationFunctionType
+ALU = mybir.AluOpType
+
+P = 128
+PACK = 4
+
+
+def tile_list_gatedtwo_twotab_one_tabled_kernel(
+    tc, xt_words, xt_scales, w_words, w_scales, xo_words, xo_scales, w2_words, w2_scales,
+    sg, bg, wb_words, wb_scales, tz, offs, offs2, offs3, offs4, offs5, offs6, out,
+):
+    nc = tc.nc
+    with ExitStack() as ctx:
+        keep = ctx.enter_context(tc.tile_pool(name="keep", bufs=1))
+        psum = ctx.enter_context(tc.psum_pool(name="psum", bufs=4))
+
+        def sbuf(name, shape, dtype):
+            return keep.tile(shape, dtype, name=name, align_bytes=64)
+
+        def load_list(name, source):
+            tile = keep.tile(list(source.shape), U16, name=name)
+            nc.sync.dma_start(tile[:], source)
+            return tile
+
+        def load_words(name, source, columns):
+            tile = sbuf(name, [P, columns], U32)
+            nc.sync.dma_start(tile[:].bitcast(I32), source[0].rearrange("p c t -> p (c t)").bitcast(I32))
+            return tile
+
+        def zeroed_plane(name, columns, engine):
+            tile = sbuf(name, [P, columns], U8)
+            engine.memset(tile[:].bitcast(I32), 0)
+            return tile
+
+        def load_scales(tile, source, queues):
+            for q, queue in enumerate(queues):
+                queue.dma_start(
+                    tile[32 * q : 32 * q + 4, :].bitcast(I32),
+                    source[0, 4 * q : 4 * q + 4, :].bitcast(I32),
+                )
+
+        def deal(copy, dealt, source, run):
+            copy(
+                dealt[:].rearrange("p t (c i) -> p c t i", i=run),
+                source.rearrange("p (c i t) -> p c t i", i=run, t=PACK),
+            )
+
+        xt_plane = zeroed_plane("xt_plane", T, nc.vector)
+        w_plane = zeroed_plane("w_plane", R, nc.vector)
+        xo_plane = zeroed_plane("xo_plane", Z, nc.vector)
+        w2_plane = zeroed_plane("w2_plane", R, nc.vector)
+        wb_plane = zeroed_plane("wb_plane", N, nc.vector)
+
+        slope = sbuf("slope", [P, PACK], F32)
+        nc.gpsimd.dma_start(slope[:], sg.rearrange("(p t) o -> p (t o)", t=PACK))
+        offset = sbuf("offset", [P, PACK], F32)
+        nc.gpsimd.dma_start(offset[:], bg.rearrange("(p t) o -> p (t o)", t=PACK))
+
+        list1 = load_list("list1", offs)
+        xt_tab = sbuf("xt_tab", [P, T], U16)
+        nc.sync.dma_start(xt_tab[:].bitcast(I32), xt_words[0].bitcast(I32))
+        w_tab = load_words("w_tab", w_words, R)
+        load_scales(xt_plane, xt_scales, [nc.scalar] * 4)
+        load_scales(w_plane, w_scales, [nc.sync] * 4)
+        xo_tab = load_words("xo_tab", xo_words, Z)
+        list2 = load_list("list2", offs2)
+        list3 = load_list("list3", offs3)
+        load_scales(xo_plane, xo_scales, [nc.sync] * 4)
+        w2_tab = load_words("w2_tab", w2_words, R)
+        load_scales(w2_plane, w2_scales, [nc.sync, nc.sync, nc.gpsimd, nc.gpsimd])
+        list4 = load_list("list4", offs4)
+        list5 = load_list("list5", offs5)
+        wb_tab = load_words("wb_tab", wb_words, N)
+        list6 = load_list("list6", offs6)
+        tz_tab = sbuf("tz_tab", [P, 2, E], F32)
+        nc.sync.dma_start(tz_tab[:], tz.rearrange("(h p) e -> p h e", p=P))
+        load_scales(wb_plane, wb_scales, [nc.sync] * 4)
+
+        xt_codes = sbuf("xt_codes", [P, J], U16)
+        nc.vector.tensor_copy(xt_codes[:], xt_tab[:].indirect(list1[:]))
+        w_codes = sbuf("w_codes", [P, PACK, P], U32)
+        deal(nc.scalar.copy, w_codes, w_tab[:], 4)
+        xt_bytes = sbuf("xt_bytes", [P, J], U8)
+        nc.vector.tensor_copy(xt_bytes[:], xt_plane[:].indirect(list1[:]))
+        w_bytes = sbuf("w_bytes", [P, PACK, P], U8)
+        deal(nc.vector.tensor_copy, w_bytes, w_plane[:], 16)
+        a_sum = []
+        for t in range(PACK):
+            bank = psum.tile([P, J], F32, name="a_sum", tag="first")
+            nc.tensor.matmul_mx(
+                bank[:], lhsT=w_codes[:, t, :].bitcast(E5M2), lhsT_scale=w_bytes[:, t, :],
+                rhs=xt_codes[:].bitcast(E2M1), rhs_scale=xt_bytes[:], start=True, stop=True,
+            )
+            a_sum.append(bank)
+
+        xo_codes = sbuf("xo_codes", [P, J], U32)
+        nc.vector.tensor_copy(xo_codes[:], xo_tab[:].indirect(list2[:]))
+        w2_codes = sbuf("w2_codes", [P, PACK, P], U32)
+        deal(nc.scalar.copy, w2_codes, w2_tab[:], 4)
+        xo_bytes = sbuf("xo_bytes", [P, J], U8)
+        nc.vector.tensor_copy(xo_bytes[:], xo_plane[:].indirect(list2[:]))
+        w2_bytes = sbuf("w2_bytes", [P, PACK, P], U8)
+        deal(nc.vector.tensor_copy, w2_bytes, w2_plane[:], 16)
+        b_sum = []
+        for t in range(PACK):
+            bank = psum.tile([P, J], F32, name="b_sum", tag="second")
+            nc.tensor.matmul_mx(
+                bank[:], lhsT=w2_codes[:, t, :].bitcast(E4M3), lhsT_scale=w2_bytes[:, t, :],
+                rhs=xo_codes[:].bitcast(E5M2), rhs_scale=xo_bytes[:], start=True, stop=True,
+            )
+            b_sum.append(bank)
+
+        gate = sbuf("gate", [P, PACK, J], F32)
+        for t in range(PACK):
+            a_rows = sbuf("a_rows%d" % t, [P, J], F32)
+            if t < 2:
+                nc.scalar.copy(a_rows[:], a_sum[t][:])
+            else:
+                nc.vector.tensor_copy(a_rows[:], a_sum[t][:])
+            for half in range(2):
+                nc.scalar.activation(
+                    gate[:, t, 128 * half : 128 * (half + 1)],
+                    a_rows[:].indirect(list3[:, 8 * half : 8 * (half + 1)]),
+                    ACT.Sigmoid, bias=offset[:, t : t + 1], scale=slope[:, t : t + 1],
+                )
+
+        hg = [sbuf("hg%d" % t, [P, J], F32) for t in range(PACK)]
+        pick4 = sbuf("pick4", [P, PACK, O], F32)
+        pick5 = sbuf("pick5", [P, PACK, O], F32)
+        hid = sbuf("hid", [P, O, PACK], BF16)
+
+        def product(t):
+            nc.vector.tensor_tensor(hg[t][:], b_sum[t][:], gate[:, t, :], ALU.mult)
+
+        def picks(t):
+            nc.vector.tensor_copy(pick4[:, t, :], hg[t][:].indirect(list4[:]))
+            nc.scalar.activation(pick5[:, t, :], hg[t][:].indirect(list5[:]), ACT.Copy)
+
+        def larger(u):
+            nc.vector.tensor_tensor(
+                hid[:, :, 2 * u : 2 * u + 2],
+                pick4[:, 2 * u : 2 * u + 2, :].rearrange("p t o -> p o t"),
+                pick5[:, 2 * u : 2 * u + 2, :].rearrange("p t o -> p o t"),
+                ALU.max,
+            )
+
+        product(0)
+        for t in range(1, PACK):
+            product(t)
+            picks(t - 1)
+        larger(0)
+        picks(PACK - 1)
+        larger(1)
+
+        tz_pick = sbuf("tz_pick", [P, 2, O], F32)
+        for h in range(2):
+            nc.scalar.activation(tz_pick[:, h, :], tz_tab[:, h, :].indirect(list6[:]), ACT.Copy)
+
+        hid_codes = sbuf("hid_codes", [P, O], U32)
+        hid_bytes = sbuf("hid_bytes", [P, O], U8)
+        nc.vector.quantize_mx(
+            out=hid_codes[:].bitcast(E5M2), scales=hid_bytes[:],
+            in_=hid[:].rearrange("p o t -> p (o t)"),
+        )
+        p_sum = psum.tile([P, 2, O], F32, name="p_sum", tag="first")
+        for h in range(2):
+            nc.tensor.matmul_mx(
+                p_sum[:, h, :], lhsT=wb_tab[:, P * h : P * (h + 1)].bitcast(E4M3),
+                lhsT_scale=wb_plane[:, P * h : P * (h + 1)],
+                rhs=hid_codes[:].bitcast(E5M2), rhs_scale=hid_bytes[:], start=True, stop=True,
+            )
+        result = sbuf("result", [P, 2, O], F32)
+        nc.vector.tensor_tensor(result[:], p_sum[:], tz_pick[:], ALU.add)
+        nc.sync.dma_start(out.rearrange("(h p) o -> p h o", p=P), result[:])

@@ -19,6 +19,11 @@ ALU = mybir.AluOpType
 
 P = 128
 PACK = 4
+QUADRANTS = 4
+LINE_BYTES = 16
+LIST_ROWS = 16
+GATE_PIECES = 2
+A_COPIES_ON_VECTOR = 2
 
 
 def tile_list_gatedtwo_twotab_one_tabled_kernel(
@@ -28,7 +33,7 @@ def tile_list_gatedtwo_twotab_one_tabled_kernel(
     nc = tc.nc
     with ExitStack() as ctx:
         keep = ctx.enter_context(tc.tile_pool(name="keep", bufs=1))
-        psum = ctx.enter_context(tc.psum_pool(name="psum", bufs=4))
+        psum = ctx.enter_context(tc.psum_pool(name="psum", bufs=PACK))
 
         def sbuf(name, shape, dtype):
             return keep.tile(shape, dtype, name=name, align_bytes=64)
@@ -43,29 +48,30 @@ def tile_list_gatedtwo_twotab_one_tabled_kernel(
             nc.sync.dma_start(tile[:].bitcast(I32), source[0].rearrange("p c t -> p (c t)").bitcast(I32))
             return tile
 
-        def zeroed_plane(name, columns, engine):
+        def zeroed_plane(name, columns):
             tile = sbuf(name, [P, columns], U8)
-            engine.memset(tile[:].bitcast(I32), 0)
+            nc.vector.memset(tile[:].bitcast(I32), 0)
             return tile
 
-        def load_scales(tile, source, queues):
+        def load_plane(tile, source, queues):
             for q, queue in enumerate(queues):
                 queue.dma_start(
                     tile[32 * q : 32 * q + 4, :].bitcast(I32),
                     source[0, 4 * q : 4 * q + 4, :].bitcast(I32),
                 )
 
-        def deal(copy, dealt, source, run):
-            copy(
+        def deal(dealt, source, element_bytes):
+            run = LINE_BYTES // element_bytes
+            nc.vector.tensor_copy(
                 dealt[:].rearrange("p t (c i) -> p c t i", i=run),
-                source.rearrange("p (c i t) -> p c t i", i=run, t=PACK),
+                source[:].rearrange("p (c i t) -> p c t i", i=run, t=PACK),
             )
 
-        xt_plane = zeroed_plane("xt_plane", T, nc.vector)
-        w_plane = zeroed_plane("w_plane", R, nc.vector)
-        xo_plane = zeroed_plane("xo_plane", Z, nc.vector)
-        w2_plane = zeroed_plane("w2_plane", R, nc.vector)
-        wb_plane = zeroed_plane("wb_plane", N, nc.vector)
+        xt_plane = zeroed_plane("xt_plane", T)
+        w_plane = zeroed_plane("w_plane", R)
+        xo_plane = zeroed_plane("xo_plane", Z)
+        w2_plane = zeroed_plane("w2_plane", R)
+        wb_plane = zeroed_plane("wb_plane", N)
 
         slope = sbuf("slope", [P, PACK], F32)
         nc.gpsimd.dma_start(slope[:], sg.rearrange("(p t) o -> p (t o)", t=PACK))
@@ -76,33 +82,38 @@ def tile_list_gatedtwo_twotab_one_tabled_kernel(
         xt_tab = sbuf("xt_tab", [P, T], U16)
         nc.sync.dma_start(xt_tab[:].bitcast(I32), xt_words[0].bitcast(I32))
         w_tab = load_words("w_tab", w_words, R)
-        load_scales(xt_plane, xt_scales, [nc.scalar] * 4)
-        load_scales(w_plane, w_scales, [nc.sync] * 4)
+        load_plane(xt_plane, xt_scales, [nc.scalar] * QUADRANTS)
+        load_plane(w_plane, w_scales, [nc.sync] * QUADRANTS)
         xo_tab = load_words("xo_tab", xo_words, Z)
         list2 = load_list("list2", offs2)
         list3 = load_list("list3", offs3)
-        load_scales(xo_plane, xo_scales, [nc.sync] * 4)
+        load_plane(xo_plane, xo_scales, [nc.sync] * QUADRANTS)
         w2_tab = load_words("w2_tab", w2_words, R)
-        load_scales(w2_plane, w2_scales, [nc.sync, nc.sync, nc.gpsimd, nc.gpsimd])
+        load_plane(w2_plane, w2_scales, [nc.sync, nc.sync, nc.gpsimd, nc.gpsimd])
         list4 = load_list("list4", offs4)
         list5 = load_list("list5", offs5)
         wb_tab = load_words("wb_tab", wb_words, N)
         list6 = load_list("list6", offs6)
-        tz_tab = sbuf("tz_tab", [P, 2, E], F32)
+        tz_tab = sbuf("tz_tab", [P, N // P, E], F32)
         nc.sync.dma_start(tz_tab[:], tz.rearrange("(h p) e -> p h e", p=P))
-        load_scales(wb_plane, wb_scales, [nc.sync] * 4)
+        load_plane(wb_plane, wb_scales, [nc.sync] * QUADRANTS)
+
+        warm_in = sbuf("warm_in", [P, 1], F32)
+        nc.vector.memset(warm_in[:], 0.0)
+        warm_out = sbuf("warm_out", [P, 1], F32)
+        nc.scalar.activation(warm_out[:], warm_in[:], ACT.Sigmoid)
 
         xt_codes = sbuf("xt_codes", [P, J], U16)
-        nc.vector.tensor_copy(xt_codes[:], xt_tab[:].indirect(list1[:]))
         w_codes = sbuf("w_codes", [P, PACK, P], U32)
-        deal(nc.scalar.copy, w_codes, w_tab[:], 4)
         xt_bytes = sbuf("xt_bytes", [P, J], U8)
-        nc.vector.tensor_copy(xt_bytes[:], xt_plane[:].indirect(list1[:]))
         w_bytes = sbuf("w_bytes", [P, PACK, P], U8)
-        deal(nc.vector.tensor_copy, w_bytes, w_plane[:], 16)
+        nc.vector.tensor_copy(xt_codes[:], xt_tab[:].indirect(list1[:]))
+        deal(w_codes, w_tab, 4)
+        nc.vector.tensor_copy(xt_bytes[:], xt_plane[:].indirect(list1[:]))
+        deal(w_bytes, w_plane, 1)
         a_sum = []
         for t in range(PACK):
-            bank = psum.tile([P, J], F32, name="a_sum", tag="first")
+            bank = psum.tile([P, J], F32, name="a_sum", tag="a_then_p")
             nc.tensor.matmul_mx(
                 bank[:], lhsT=w_codes[:, t, :].bitcast(E5M2), lhsT_scale=w_bytes[:, t, :],
                 rhs=xt_codes[:].bitcast(E2M1), rhs_scale=xt_bytes[:], start=True, stop=True,
@@ -110,16 +121,16 @@ def tile_list_gatedtwo_twotab_one_tabled_kernel(
             a_sum.append(bank)
 
         xo_codes = sbuf("xo_codes", [P, J], U32)
-        nc.vector.tensor_copy(xo_codes[:], xo_tab[:].indirect(list2[:]))
         w2_codes = sbuf("w2_codes", [P, PACK, P], U32)
-        deal(nc.scalar.copy, w2_codes, w2_tab[:], 4)
         xo_bytes = sbuf("xo_bytes", [P, J], U8)
-        nc.vector.tensor_copy(xo_bytes[:], xo_plane[:].indirect(list2[:]))
         w2_bytes = sbuf("w2_bytes", [P, PACK, P], U8)
-        deal(nc.vector.tensor_copy, w2_bytes, w2_plane[:], 16)
+        nc.vector.tensor_copy(xo_codes[:], xo_tab[:].indirect(list2[:]))
+        nc.vector.tensor_copy(xo_bytes[:], xo_plane[:].indirect(list2[:]))
+        deal(w2_codes, w2_tab, 4)
+        deal(w2_bytes, w2_plane, 1)
         b_sum = []
         for t in range(PACK):
-            bank = psum.tile([P, J], F32, name="b_sum", tag="second")
+            bank = psum.tile([P, J], F32, name="b_sum", tag="b")
             nc.tensor.matmul_mx(
                 bank[:], lhsT=w2_codes[:, t, :].bitcast(E4M3), lhsT_scale=w2_bytes[:, t, :],
                 rhs=xo_codes[:].bitcast(E5M2), rhs_scale=xo_bytes[:], start=True, stop=True,
@@ -127,16 +138,17 @@ def tile_list_gatedtwo_twotab_one_tabled_kernel(
             b_sum.append(bank)
 
         gate = sbuf("gate", [P, PACK, J], F32)
+        piece = J // GATE_PIECES
         for t in range(PACK):
             a_rows = sbuf("a_rows%d" % t, [P, J], F32)
-            if t < 2:
-                nc.scalar.copy(a_rows[:], a_sum[t][:])
-            else:
+            if t < A_COPIES_ON_VECTOR:
                 nc.vector.tensor_copy(a_rows[:], a_sum[t][:])
-            for half in range(2):
+            else:
+                nc.scalar.copy(a_rows[:], a_sum[t][:])
+            for g in range(GATE_PIECES):
+                entries = list3[:, g * piece // LIST_ROWS : (g + 1) * piece // LIST_ROWS]
                 nc.scalar.activation(
-                    gate[:, t, 128 * half : 128 * (half + 1)],
-                    a_rows[:].indirect(list3[:, 8 * half : 8 * (half + 1)]),
+                    gate[:, t, g * piece : (g + 1) * piece], a_rows[:].indirect(entries),
                     ACT.Sigmoid, bias=offset[:, t : t + 1], scale=slope[:, t : t + 1],
                 )
 
@@ -148,9 +160,11 @@ def tile_list_gatedtwo_twotab_one_tabled_kernel(
         def product(t):
             nc.vector.tensor_tensor(hg[t][:], b_sum[t][:], gate[:, t, :], ALU.mult)
 
-        def picks(t):
-            nc.vector.tensor_copy(pick4[:, t, :], hg[t][:].indirect(list4[:]))
-            nc.scalar.activation(pick5[:, t, :], hg[t][:].indirect(list5[:]), ACT.Copy)
+        def pick_on_vector(picked, places, t):
+            nc.vector.tensor_copy(picked[:, t, :], hg[t][:].indirect(places[:]))
+
+        def pick_on_scalar(picked, places, t):
+            nc.scalar.activation(picked[:, t, :], hg[t][:].indirect(places[:]), ACT.Copy)
 
         def larger(u):
             nc.vector.tensor_tensor(
@@ -161,15 +175,22 @@ def tile_list_gatedtwo_twotab_one_tabled_kernel(
             )
 
         product(0)
-        for t in range(1, PACK):
-            product(t)
-            picks(t - 1)
+        product(1)
+        pick_on_vector(pick4, list4, 0)
+        product(2)
+        pick_on_vector(pick5, list5, 0)
+        pick_on_scalar(pick5, list5, 1)
+        product(3)
+        pick_on_vector(pick4, list4, 1)
+        pick_on_scalar(pick4, list4, 2)
+        pick_on_scalar(pick5, list5, 2)
         larger(0)
-        picks(PACK - 1)
+        pick_on_scalar(pick5, list5, 3)
+        pick_on_vector(pick4, list4, 3)
         larger(1)
 
-        tz_pick = sbuf("tz_pick", [P, 2, O], F32)
-        for h in range(2):
+        tz_pick = keep.tile([P, N // P, O], F32, name="tz_pick", tag="hg%d" % (PACK - 1), align_bytes=64)
+        for h in range(N // P):
             nc.scalar.activation(tz_pick[:, h, :], tz_tab[:, h, :].indirect(list6[:]), ACT.Copy)
 
         hid_codes = sbuf("hid_codes", [P, O], U32)
@@ -178,13 +199,14 @@ def tile_list_gatedtwo_twotab_one_tabled_kernel(
             out=hid_codes[:].bitcast(E5M2), scales=hid_bytes[:],
             in_=hid[:].rearrange("p o t -> p (o t)"),
         )
-        p_sum = psum.tile([P, 2, O], F32, name="p_sum", tag="first")
-        for h in range(2):
+
+        for h, queue in enumerate((nc.sync, nc.scalar)):
+            rows = slice(P * h, P * (h + 1))
+            p_sum = psum.tile([P, O], F32, name="p_sum", tag="a_then_p")
             nc.tensor.matmul_mx(
-                p_sum[:, h, :], lhsT=wb_tab[:, P * h : P * (h + 1)].bitcast(E4M3),
-                lhsT_scale=wb_plane[:, P * h : P * (h + 1)],
+                p_sum[:], lhsT=wb_tab[:, rows].bitcast(E4M3), lhsT_scale=wb_plane[:, rows],
                 rhs=hid_codes[:].bitcast(E5M2), rhs_scale=hid_bytes[:], start=True, stop=True,
             )
-        result = sbuf("result", [P, 2, O], F32)
-        nc.vector.tensor_tensor(result[:], p_sum[:], tz_pick[:], ALU.add)
-        nc.sync.dma_start(out.rearrange("(h p) o -> p h o", p=P), result[:])
+            result = sbuf("result%d" % h, [P, O], F32)
+            nc.vector.tensor_tensor(result[:], p_sum[:], tz_pick[:, h, :], ALU.add)
+            queue.dma_start(out[rows, :], result[:])

from contextlib import ExitStack

import concourse.mybir as mybir

K, F, T, Z, J, R, O, N, E = 512, 512, 1024, 1024, 256, 512, 128, 256, 1024
FLOPS = 2 * K * R * J + 2 * F * R * J + 2 * R * N * O

F32 = mybir.dt.float32
BF16 = mybir.dt.bfloat16
I32 = mybir.dt.int32
U32 = mybir.dt.uint32
U16 = mybir.dt.uint16
U8 = mybir.dt.uint8
E4M3 = mybir.dt.float8_e4m3fn_x4
E5M2 = mybir.dt.float8_e5m2_x4
E2M1 = mybir.dt.float4_e2m1fn_x4
ACT = mybir.ActivationFunctionType
ALU = mybir.AluOpType

P = 128
PACK = 4
QUADRANTS = 4
LINE_BYTES = 16
LIST_ROWS = 16
GATE_PIECES = 2
A_COPIES_ON_VECTOR = 2


def tile_list_gatedtwo_twotab_one_tabled_kernel(
    tc, xt_words, xt_scales, w_words, w_scales, xo_words, xo_scales, w2_words, w2_scales,
    sg, bg, wb_words, wb_scales, tz, offs, offs2, offs3, offs4, offs5, offs6, out,
):
    nc = tc.nc
    with ExitStack() as ctx:
        keep = ctx.enter_context(tc.tile_pool(name="keep", bufs=1))
        psum = ctx.enter_context(tc.psum_pool(name="psum", bufs=PACK))

        def sbuf(name, shape, dtype):
            return keep.tile(shape, dtype, name=name, align_bytes=64)

        def load_list(name, source):
            tile = keep.tile(list(source.shape), U16, name=name)
            nc.sync.dma_start(tile[:], source)
            return tile

        def load_words(name, source, columns):
            tile = sbuf(name, [P, columns], U32)
            nc.sync.dma_start(tile[:].bitcast(I32), source[0].rearrange("p c t -> p (c t)").bitcast(I32))
            return tile

        def zeroed_plane(name, columns):
            tile = sbuf(name, [P, columns], U8)
            nc.vector.memset(tile[:].bitcast(I32), 0)
            return tile

        def load_plane(tile, source, queues):
            for q, queue in enumerate(queues):
                queue.dma_start(
                    tile[32 * q : 32 * q + 4, :].bitcast(I32),
                    source[0, 4 * q : 4 * q + 4, :].bitcast(I32),
                )

        def deal(dealt, source, element_bytes):
            run = LINE_BYTES // element_bytes
            nc.vector.tensor_copy(
                dealt[:].rearrange("p t (c i) -> p c t i", i=run),
                source[:].rearrange("p (c i t) -> p c t i", i=run, t=PACK),
            )

        xt_plane = zeroed_plane("xt_plane", T)
        w_plane = zeroed_plane("w_plane", R)
        xo_plane = zeroed_plane("xo_plane", Z)
        w2_plane = zeroed_plane("w2_plane", R)
        wb_plane = zeroed_plane("wb_plane", N)

        slope = sbuf("slope", [P, PACK], F32)
        nc.gpsimd.dma_start(slope[:], sg.rearrange("(p t) o -> p (t o)", t=PACK))
        offset = sbuf("offset", [P, PACK], F32)
        nc.gpsimd.dma_start(offset[:], bg.rearrange("(p t) o -> p (t o)", t=PACK))

        list1 = load_list("list1", offs)
        xt_tab = sbuf("xt_tab", [P, T], U16)
        nc.sync.dma_start(xt_tab[:].bitcast(I32), xt_words[0].bitcast(I32))
        w_tab = load_words("w_tab", w_words, R)
        load_plane(xt_plane, xt_scales, [nc.scalar] * QUADRANTS)
        load_plane(w_plane, w_scales, [nc.sync] * QUADRANTS)
        xo_tab = load_words("xo_tab", xo_words, Z)
        list2 = load_list("list2", offs2)
        list3 = load_list("list3", offs3)
        load_plane(xo_plane, xo_scales, [nc.sync] * QUADRANTS)
        w2_tab = load_words("w2_tab", w2_words, R)
        load_plane(w2_plane, w2_scales, [nc.sync, nc.sync, nc.gpsimd, nc.gpsimd])
        list4 = load_list("list4", offs4)
        list5 = load_list("list5", offs5)
        wb_tab = load_words("wb_tab", wb_words, N)
        list6 = load_list("list6", offs6)
        tz_tab = sbuf("tz_tab", [P, N // P, E], F32)
        nc.sync.dma_start(tz_tab[:], tz.rearrange("(h p) e -> p h e", p=P))
        load_plane(wb_plane, wb_scales, [nc.sync] * QUADRANTS)

        warm_in = sbuf("warm_in", [P, 1], F32)
        nc.vector.memset(warm_in[:], 0.0)
        warm_out = sbuf("warm_out", [P, 1], F32)
        nc.scalar.activation(warm_out[:], warm_in[:], ACT.Sigmoid)

        xt_codes = sbuf("xt_codes", [P, J], U16)
        w_codes = sbuf("w_codes", [P, PACK, P], U32)
        xt_bytes = sbuf("xt_bytes", [P, J], U8)
        w_bytes = sbuf("w_bytes", [P, PACK, P], U8)
        nc.vector.tensor_copy(xt_codes[:], xt_tab[:].indirect(list1[:]))
        deal(w_codes, w_tab, 4)
        nc.vector.tensor_copy(xt_bytes[:], xt_plane[:].indirect(list1[:]))
        deal(w_bytes, w_plane, 1)
        a_sum = []
        for t in range(PACK):
            bank = psum.tile([P, J], F32, name="a_sum", tag="a_then_p")
            nc.tensor.matmul_mx(
                bank[:], lhsT=w_codes[:, t, :].bitcast(E5M2), lhsT_scale=w_bytes[:, t, :],
                rhs=xt_codes[:].bitcast(E2M1), rhs_scale=xt_bytes[:], start=True, stop=True,
            )
            a_sum.append(bank)

        xo_codes = sbuf("xo_codes", [P, J], U32)
        w2_codes = sbuf("w2_codes", [P, PACK, P], U32)
        xo_bytes = sbuf("xo_bytes", [P, J], U8)
        w2_bytes = sbuf("w2_bytes", [P, PACK, P], U8)
        nc.vector.tensor_copy(xo_codes[:], xo_tab[:].indirect(list2[:]))
        nc.vector.tensor_copy(xo_bytes[:], xo_plane[:].indirect(list2[:]))
        deal(w2_codes, w2_tab, 4)
        deal(w2_bytes, w2_plane, 1)
        b_sum = []
        for t in range(PACK):
            bank = psum.tile([P, J], F32, name="b_sum", tag="b")
            nc.tensor.matmul_mx(
                bank[:], lhsT=w2_codes[:, t, :].bitcast(E4M3), lhsT_scale=w2_bytes[:, t, :],
                rhs=xo_codes[:].bitcast(E5M2), rhs_scale=xo_bytes[:], start=True, stop=True,
            )
            b_sum.append(bank)

        gate = sbuf("gate", [P, PACK, J], F32)
        piece = J // GATE_PIECES
        for t in range(PACK):
            a_rows = sbuf("a_rows%d" % t, [P, J], F32)
            if t < A_COPIES_ON_VECTOR:
                nc.vector.tensor_copy(a_rows[:], a_sum[t][:])
            else:
                nc.scalar.copy(a_rows[:], a_sum[t][:])
            for g in range(GATE_PIECES):
                entries = list3[:, g * piece // LIST_ROWS : (g + 1) * piece // LIST_ROWS]
                nc.scalar.activation(
                    gate[:, t, g * piece : (g + 1) * piece], a_rows[:].indirect(entries),
                    ACT.Sigmoid, bias=offset[:, t : t + 1], scale=slope[:, t : t + 1],
                )

        hg = [sbuf("hg%d" % t, [P, J], F32) for t in range(PACK)]
        pick4 = sbuf("pick4", [P, PACK, O], F32)
        pick5 = sbuf("pick5", [P, PACK, O], F32)
        hid = sbuf("hid", [P, O, PACK], BF16)

        def product(t):
            nc.vector.tensor_tensor(hg[t][:], b_sum[t][:], gate[:, t, :], ALU.mult)

        def pick_on_vector(picked, places, t):
            nc.vector.tensor_copy(picked[:, t, :], hg[t][:].indirect(places[:]))

        def pick_on_scalar(picked, places, t):
            nc.scalar.activation(picked[:, t, :], hg[t][:].indirect(places[:]), ACT.Copy)

        def larger(u):
            nc.vector.tensor_tensor(
                hid[:, :, 2 * u : 2 * u + 2],
                pick4[:, 2 * u : 2 * u + 2, :].rearrange("p t o -> p o t"),
                pick5[:, 2 * u : 2 * u + 2, :].rearrange("p t o -> p o t"),
                ALU.max,
            )

        product(0)
        product(1)
        pick_on_vector(pick4, list4, 0)
        product(2)
        pick_on_vector(pick5, list5, 0)
        pick_on_scalar(pick5, list5, 1)
        product(3)
        pick_on_vector(pick4, list4, 1)
        pick_on_scalar(pick4, list4, 2)
        pick_on_scalar(pick5, list5, 2)
        larger(0)
        pick_on_scalar(pick5, list5, 3)
        pick_on_vector(pick4, list4, 3)
        larger(1)

        tz_pick = keep.tile([P, N // P, O], F32, name="tz_pick", tag="hg%d" % (PACK - 1), align_bytes=64)
        for h in range(N // P):
            nc.scalar.activation(tz_pick[:, h, :], tz_tab[:, h, :].indirect(list6[:]), ACT.Copy)

        hid_codes = sbuf("hid_codes", [P, O], U32)
        hid_bytes = sbuf("hid_bytes", [P, O], U8)
        nc.vector.quantize_mx(
            out=hid_codes[:].bitcast(E5M2), scales=hid_bytes[:],
            in_=hid[:].rearrange("p o t -> p (o t)"),
        )

        for h, queue in enumerate((nc.sync, nc.scalar)):
            rows = slice(P * h, P * (h + 1))
            p_sum = psum.tile([P, O], F32, name="p_sum", tag="a_then_p")
            nc.tensor.matmul_mx(
                p_sum[:], lhsT=wb_tab[:, rows].bitcast(E4M3), lhsT_scale=wb_plane[:, rows],
                rhs=hid_codes[:].bitcast(E5M2), rhs_scale=hid_bytes[:], start=True, stop=True,
            )
            result = sbuf("result%d" % h, [P, O], F32)
            nc.vector.tensor_tensor(result[:], p_sum[:], tz_pick[:, h, :], ALU.add)
            queue.dma_start(out[rows, :], result[:])
